import numpy as np
import ml_dtypes


def mxq(x, axis, fmt="e4m3"):
    dtype, down = {"e4m3": (ml_dtypes.float8_e4m3fn, 7), "e5m2": (ml_dtypes.float8_e5m2, 14)}[fmt]
    v = np.moveaxis(np.asarray(x, np.float32).astype(ml_dtypes.bfloat16).astype(np.float64), axis, -1)
    blocks = v.reshape(v.shape[:-1] + (-1, 32))
    amax = np.abs(blocks).max(-1, keepdims=True)
    byte = np.maximum(np.where(amax > 0, np.frexp(amax)[1] - 1 + 127, 0) - down, 1)
    scale = np.exp2(byte - 127.0)
    codes = (blocks / scale).astype(np.float32).astype(dtype).astype(np.float64)
    return np.moveaxis((codes * scale).reshape(v.shape), -1, axis)


WIDE = False


def mx_kscale(k):
    if not WIDE:
        return np.ones(k)
    levels = np.array([10, -10, 5, -5, 0])
    if k % 512:
        return np.exp2(np.random.permutation(np.resize(levels, k // 32))).repeat(32)
    a = np.empty((k // 512, 16))
    for p in range(k // 512):
        a[p, :8] = np.random.permutation(np.resize(levels, 8))
        for g in range(8):
            far = levels[np.abs(levels - a[p, g]) >= 10]
            a[p, g + 8] = far[np.random.randint(len(far))]
    return np.exp2(a.ravel()).repeat(32)


def f64(x):
    return np.asarray(x).astype(np.float64)


def striped(idx):
    return np.tile(idx.reshape(-1, 16).T, (8, 1)).astype(np.uint16)


def unstriped(offs):
    return offs[:16].T.reshape(-1).astype(np.int64)


def striped8(idx):
    return np.concatenate([x.reshape(-1, 16).T for x in idx]).astype(np.uint16)


def runs(offs, k):
    lists = np.stack([offs[16 * r : 16 * r + 16].T.reshape(-1) for r in range(8)]).astype(np.int64)
    return lists[np.arange(k) % 512 // 64]


def pack_weight(w):
    k, n = w.shape
    w = f64(np.asarray(w, np.float32).astype(ml_dtypes.bfloat16)).reshape(k // 32, 32, n)
    amax = np.abs(w).max(1)
    byte = np.clip(np.where(amax > 0, np.frexp(amax)[1] - 1 + 127 - 7, 1), 1, 254)
    scaled = (w * np.exp2(127.0 - byte)[:, None, :]).reshape(k, n).astype(np.float32)
    words = np.ascontiguousarray(scaled.reshape(k // 512, 128, 4, n).transpose(0, 1, 3, 2)).astype(ml_dtypes.float8_e4m3fn).view(np.uint8)
    return words, np.ascontiguousarray(byte.astype(np.uint8).reshape(k // 512, 16, n))


def unpack_weight(words, scales):
    g, p, n, _ = words.shape
    vals = np.ascontiguousarray(words).view(ml_dtypes.float8_e4m3fn).astype(np.float64) * np.repeat(np.exp2(scales.astype(np.float64) - 127.0), 8, axis=1)[..., None]
    return vals.transpose(0, 1, 3, 2).reshape(g * 512, n)


E2M1 = np.array([0.0, 0.5, 1.0, 1.5, 2.0, 3.0, 4.0, 6.0, -0.0, -0.5, -1.0, -1.5, -2.0, -3.0, -4.0, -6.0])


def pack_fp4(w):
    k, n = w.shape
    w = f64(np.asarray(w, np.float32).astype(ml_dtypes.bfloat16)).reshape(k // 32, 32, n)
    amax = np.abs(w).max(1)
    mant, ex = np.frexp(amax / 6.0)
    byte = np.clip(np.where(amax > 0, np.where(mant > 0.5, ex, ex - 1) + 127, 1), 1, 254)
    scaled = (w * np.exp2(127.0 - byte)[:, None, :]).reshape(k, n).astype(np.float32)
    c = np.ascontiguousarray(scaled.reshape(k // 512, 128, 4, n).transpose(0, 1, 3, 2)).astype(ml_dtypes.float4_e2m1fn).view(np.uint8) & 0xF
    words = (c[..., 0::2] | (c[..., 1::2] << 4)).reshape(k // 512, 128, 2 * n)
    return np.ascontiguousarray(words), np.ascontiguousarray(byte.astype(np.uint8).reshape(k // 512, 16, n))


def unpack_fp4(words, scales):
    g, _, n = scales.shape
    words = np.ascontiguousarray(words).reshape(g, 128, n, 2)
    nib = np.empty((g, 128, n, 4), np.uint8)
    nib[..., 0::2] = words & 0xF
    nib[..., 1::2] = words >> 4
    vals = E2M1[nib] * np.repeat(np.exp2(scales.astype(np.float64) - 127.0), 8, axis=1)[..., None]
    return vals.transpose(0, 1, 3, 2).reshape(g * 512, n)


def sigmoid(v):
    return 1.0 / (1.0 + np.exp(-np.maximum(v, -700.0)))

def planes(y):
    n, m = y.shape
    v = y.astype(np.float32).astype(ml_dtypes.bfloat16).astype(np.float64).reshape(n // 32, 32, m)
    top = np.abs(v).max(1)
    byte = np.clip(np.where(top > 0, np.frexp(top)[1] - 1 + 127 - 7, 1), 1, 254)
    codes = (v * np.exp2(127.0 - byte)[:, None, :]).reshape(n, m).astype(np.float32).astype(ml_dtypes.float8_e4m3fn).view(np.uint8)
    words = codes.reshape(n // 512, 128, 4, m).transpose(0, 1, 3, 2)
    return np.ascontiguousarray(words), np.ascontiguousarray(byte.astype(np.uint8).reshape(n // 512, 16, m))


K, T, S, N, H, G, U = 512, 2048, 512, 512, 512, 2048, 1024


def setup_inputs():
    n = np.random.standard_normal
    s = mx_kscale(K)[:, None]
    u = mx_kscale(S)
    packed_xT = pack_weight(n((K, T)) * s)
    packed_w1 = pack_fp4(n((K, H)) / np.sqrt(K) / s)
    packed_dT = pack_weight(n((K, G)) / s)
    packed_w2 = pack_fp4(n((H, N)) / np.sqrt(H) / u[:, None])
    return {
        "x_words": packed_xT[0],
        "x_scales": packed_xT[1],
        "w1_words": packed_w1[0],
        "w1_scales": packed_w1[1],
        "d_words": packed_dT[0],
        "d_scales": packed_dT[1],
        "gn": (np.random.uniform(0.5, 1.5, (H, 1)) * u[:, None]).astype(np.float32),
        "w2_words": packed_w2[0],
        "w2_scales": packed_w2[1],
        "mem": n((N, U)).astype(np.float32),
        "offs": striped(np.random.permutation(T)[:S]),
        "k1": striped8(np.random.randint(0, G, (8, H))),
        "two": striped(np.random.permutation(T)[:S]),
        "n1": striped8(np.stack([np.random.permutation(S) for _ in range(8)])),
        "n2": striped8(np.stack([np.random.permutation(S) for _ in range(8)])),
        "n3": striped8(np.stack([np.random.permutation(U)[:S] for _ in range(8)])),
    }


def reference(x_words, x_scales, w1_words, w1_scales, d_words, d_scales, gn, w2_words, w2_scales, mem, offs, k1, two, n1, n2, n3):
    old = f64(mem)[np.arange(N)[:, None], runs(n3, N)]
    xq = unpack_weight(x_words, x_scales)[:, unstriped(offs)]
    y = unpack_fp4(w1_words, w1_scales).T @ xq
    d_k1 = unpack_weight(d_words, d_scales)[np.arange(K)[:, None], runs(k1, K)]
    x_two = unpack_weight(x_words, x_scales)[:, unstriped(two)]
    d = 0.0625 * (d_k1.T @ x_two)
    z = f64(gn) * (y * (np.tanh(d[np.arange(H)[:, None], runs(n1, H)] - (d[np.arange(H)[:, None], runs(n2, H)]))))
    h = unpack_fp4(w2_words, w2_scales).T @ mxq(z, 0, "e4m3")
    nw = old + sigmoid(h) * (h - old)
    out = f64(mem).copy()
    out[np.arange(N)[:, None], runs(n3, N)] = nw
    return (out,) + planes(out)

@@ -1,0 +1,269 @@
+from contextlib import ExitStack
+
+import concourse.mybir as mybir
+
+K, T, S, N, H, G, U = 512, 2048, 512, 512, 512, 2048, 1024
+FLOPS = 3 * 2 * 512 * 512 * 512
+
+F32 = mybir.dt.float32
+BF16 = mybir.dt.bfloat16
+I32 = mybir.dt.int32
+U32 = mybir.dt.uint32
+U16 = mybir.dt.uint16
+U8 = mybir.dt.uint8
+FP8X4 = mybir.dt.float8_e4m3fn_x4
+FP4X4 = mybir.dt.float4_e2m1fn_x4
+ACT = mybir.ActivationFunctionType
+ALU = mybir.AluOpType
+
+P = 128
+PACK = 4
+CH = 256
+NCH = S // CH
+
+
+def tile_picked_twkeyjointbpaget_none_po_kernel(
+    tc, x_words, x_scales, w1_words, w1_scales, d_words, d_scales, gn, w2_words, w2_scales, mem,
+    offs, k1, two, n1, n2, n3, out_0, out_1, out_2,
+):
+    nc = tc.nc
+    with ExitStack() as ctx:
+        lists = ctx.enter_context(tc.tile_pool(name="lists", bufs=1))
+        sb = ctx.enter_context(tc.tile_pool(name="sb", bufs=1))
+        psum = ctx.enter_context(tc.psum_pool(name="psum", bufs=1))
+
+        def tile(shape, dtype, name):
+            return sb.tile(shape, dtype, name=name, align_bytes=64)
+
+        def tagged(shape, dtype, name, tag):
+            return sb.tile(shape, dtype, name=name, tag=tag, align_bytes=64)
+
+        def load_list(src, name):
+            t = lists.tile([P, S // 16], U16, name=name)
+            nc.sync.dma_start(t[:], src)
+            return t
+
+        def zero(engine, t):
+            engine.memset(t[:].bitcast(I32), 0)
+
+        def dealt(ap):
+            return ap.rearrange("p (t m) -> p m t", t=PACK)
+
+        def natural(ap):
+            return ap.rearrange("p (m t) -> p m t", t=PACK)
+
+        def load_scale_rows(queue, dst, src):
+            for q in range(4):
+                queue.dma_start(dst[32 * q : 32 * q + 4, :].bitcast(I32), src[0, 4 * q : 4 * q + 4, :].bitcast(I32))
+
+        ds_win = tile([P, G], U8, "ds_win")
+        xs_win = tile([P, T], U8, "xs_win")
+        dk_plane = tile([P, H], U8, "dk_plane")
+        w1s_raw = tile([P, H], U8, "w1s_raw")
+        zero(nc.gpsimd, ds_win)
+        zero(nc.vector, xs_win)
+        zero(nc.vector, dk_plane)
+        zero(nc.gpsimd, w1s_raw)
+        w2s_raw = tile([P, N], U8, "w2s_raw")
+        zero(nc.gpsimd, w2s_raw)
+
+        k1_t = load_list(k1, "k1_t")
+        two_t = load_list(two, "two_t")
+        offs_t = load_list(offs, "offs_t")
+        n2_t = load_list(n2, "n2_t")
+        n1_t = load_list(n1, "n1_t")
+        n3_t = load_list(n3, "n3_t")
+        w1_raw = tile([P, 2 * H], U8, "w1_raw")
+        nc.sync.dma_start(w1_raw[:].bitcast(I32), w1_words[0].bitcast(I32))
+        dw_win = tile([P, G], U32, "dw_win")
+        nc.sync.dma_start(dw_win[:].bitcast(I32), d_words[0].rearrange("p n t -> p (n t)").bitcast(I32))
+        nc.sync.dma_start(ds_win[0:P:8, :].bitcast(I32), d_scales[0].bitcast(I32))
+        load_scale_rows(nc.sync, xs_win, x_scales)
+        mem_rows = mem.rearrange("(p t) u -> t p u", t=PACK)
+        page = [tile([P, U], F32, "page0"), tile([P, U], F32, "page1")]
+        nc.sync.dma_start(page[0][:], mem_rows[0])
+        xw_win = tile([P, T], U32, "xw_win")
+        nc.sync.dma_start(xw_win[:].bitcast(I32), x_words[0].rearrange("p n t -> p (n t)").bitcast(I32))
+        nc.sync.dma_start(page[1][:], mem_rows[1])
+
+        dk_s = tagged([P, H], U8, "dk_s", "slot2")
+        nc.vector.tensor_copy(dk_s[:], ds_win[:].indirect(k1_t[:]))
+        dk_s_dealt = tagged([P, H], U8, "dk_s_dealt", "slot0")
+        nc.vector.tensor_copy(dealt(dk_s_dealt[:]), natural(dk_s[:]))
+        for r in range(4):
+            nc.scalar.dma_start(dk_plane[r:P:32, :].bitcast(I32), dk_s_dealt[8 * r : P : 32, :].bitcast(I32))
+        dk_w = tile([P, H], U32, "dk_w")
+        nc.vector.tensor_copy(dk_w[:], dw_win[:].indirect(k1_t[:]))
+        dk_w_dealt = tagged([P, H], U32, "dk_w_dealt", "slot1")
+        nc.vector.tensor_copy(dealt(dk_w_dealt[:]), natural(dk_w[:]))
+        xt_s = tagged([P, S], U8, "xt_s", "slot2")
+        nc.vector.tensor_copy(xt_s[:], xs_win[:].indirect(two_t[:]))
+        xt_w = tagged([P, S], U32, "xt_w", "slot3")
+        nc.vector.tensor_copy(xt_w[:], xw_win[:].indirect(two_t[:]))
+        xq_s = tagged([P, S], U8, "xq_s", "slot0")
+        nc.vector.tensor_copy(xq_s[:], xs_win[:].indirect(offs_t[:]))
+        xq_w = tile([P, S], U32, "xq_w")
+        nc.vector.tensor_copy(xq_w[:], xw_win[:].indirect(offs_t[:]))
+
+        load_scale_rows(nc.gpsimd, w1s_raw, w1_scales)
+        gn_t = tile([P, PACK], F32, "gn_t")
+        nc.sync.dma_start(gn_t[:], gn.rearrange("(p t) o -> p (t o)", t=PACK))
+        w2_raw = tile([P, 2 * N], U8, "w2_raw")
+        nc.sync.dma_start(w2_raw[:].bitcast(I32), w2_words[0].bitcast(I32))
+        load_scale_rows(nc.gpsimd, w2s_raw, w2_scales)
+        w1_dealt = tile([P, 2 * H], U8, "w1_dealt")
+        nc.scalar.copy(dealt(w1_dealt[:].bitcast(U16)), natural(w1_raw[:].bitcast(U16)))
+        w1s = tile([P, H], U8, "w1s")
+        nc.gpsimd.tensor_copy(dealt(w1s[:]), natural(w1s_raw[:]))
+        d_ps, y_ps = [], []
+        for t in range(PACK):
+            d_ps.append(psum.tile([P, S], F32, name=f"d_ps{t}", tag=f"bank{t}"))
+            cols = slice(P * t, P * (t + 1))
+            nc.tensor.matmul_mx(out=d_ps[t][:], lhsT=dk_w_dealt[:, cols].bitcast(FP8X4), lhsT_scale=dk_plane[:, cols],
+                                rhs=xt_w[:].bitcast(FP8X4), rhs_scale=xt_s[:], start=True, stop=True)
+        w2_dealt = tile([P, 2 * N], U8, "w2_dealt")
+        nc.scalar.copy(dealt(w2_dealt[:].bitcast(U16)), natural(w2_raw[:].bitcast(U16)))
+        w2s = tile([P, N], U8, "w2s")
+        nc.gpsimd.tensor_copy(dealt(w2s[:]), natural(w2s_raw[:]))
+
+        page.append(tagged([P, U], F32, "page2", "slot1"))
+        nc.sync.dma_start(page[2][:], mem_rows[2])
+        page.append(tagged([P, U], F32, "page3", "slot3"))
+        nc.sync.dma_start(page[3][:], mem_rows[3])
+
+        def y_product(t):
+            y_ps.append(psum.tile([P, S], F32, name=f"y_ps{t}", tag=f"bank{t}"))
+            nc.tensor.matmul_mx(out=y_ps[t][:], lhsT=w1_dealt[:, 2 * P * t : 2 * P * (t + 1)].bitcast(FP4X4),
+                                lhsT_scale=w1s[:, P * t : P * (t + 1)],
+                                rhs=xq_w[:].bitcast(FP8X4), rhs_scale=xq_s[:], start=True, stop=True)
+
+        d_sb = [tile([P, S], F32, f"d_sb{t}") for t in range(PACK)]
+        d2, dd, th = {}, {}, {}
+        z_rows = [tile([P, PACK, CH], BF16, f"z_rows{c}") for c in range(NCH)]
+        z_woven = [tagged([P, CH, PACK], BF16, f"z_woven{c}", f"woven{c}") for c in range(NCH)]
+        z_w = [tile([P, CH], U32, f"z_w{c}") for c in range(NCH)]
+        z_s = [tile([P, CH], U8, f"z_s{c}") for c in range(NCH)]
+        old_half, silu_h, tanh_h, kept = {}, {}, {}, {}
+
+        def piece(lst, c):
+            return lst[:, c * CH // 16 : (c + 1) * CH // 16]
+
+        def weave(engine_copy, dst, src):
+            engine_copy(dst.rearrange("p (c i) t -> p c t i", i=4), src.rearrange("p t (c i) -> p c t i", i=4))
+
+        def evac(t):
+            if t < 3:
+                nc.scalar.copy(d_sb[t][:], d_ps[t][:])
+            else:
+                nc.vector.tensor_copy(d_sb[t][:], d_ps[t][:])
+
+        def diff(c, t):
+            nc.scalar.activation(d2[c][:, t, :], d_sb[t][:].indirect(piece(n2_t, c)), ACT.Copy)
+            nc.vector.tensor_tensor(dd[c][:, t, :], d_sb[t][:].indirect(piece(n1_t, c)), d2[c][:, t, :], ALU.subtract)
+
+        def tanh_rows(c, t0, t1):
+            nc.scalar.activation(th[c][:, t0:t1, :], dd[c][:, t0:t1, :], ACT.Tanh, scale=0.0625)
+
+        def z_row(c, t):
+            nc.vector.scalar_tensor_tensor(z_rows[c][:, t, :], y_ps[t][:, c * CH : (c + 1) * CH], gn_t[:, t : t + 1],
+                                           th[c][:, t, :], ALU.mult, ALU.mult)
+
+        def fetch_old(c, t):
+            old_half[c, t] = tagged([P, CH], F32, f"old_half{c}{t}", f"old{c}{t % 2}")
+            nc.scalar.activation(old_half[c, t][:], page[t][:].indirect(piece(n3_t, c)), ACT.Copy, scale=-0.5)
+
+        h_ps = {}
+
+        def h_product(c, copy):
+            weave(copy, z_woven[c][:], z_rows[c][:])
+            nc.vector.quantize_mx(out=z_w[c][:].bitcast(FP8X4), scales=z_s[c][:], in_=z_woven[c][:].rearrange("p c t -> p (c t)"))
+            for u in range(2):
+                h_ps[c, u] = psum.tile([P, 2, CH], F32, name=f"h_ps{c}{u}", tag=f"bank{4 + 2 * c + u}")
+                for e in range(2):
+                    t = 2 * u + e
+                    nc.tensor.matmul_mx(out=h_ps[c, u][:, e, :], lhsT=w2_dealt[:, 2 * P * t : 2 * P * (t + 1)].bitcast(FP4X4),
+                                        lhsT_scale=w2s[:, P * t : P * (t + 1)], rhs=z_w[c][:].bitcast(FP8X4), rhs_scale=z_s[c][:],
+                                        start=True, stop=True)
+
+        def h_rows(c, t):
+            return h_ps[c, t // 2][:, t % 2, :]
+
+        def keep(c, t, tag):
+            tanh_h[c, t] = tagged([P, CH], F32, f"tanh_h{c}{t}", f"ring_c{c}{t}")
+            nc.scalar.activation(tanh_h[c, t][:], h_rows(c, t), ACT.Tanh, scale=0.5)
+            kept[c, t] = tagged([P, CH], F32, f"kept{c}{t}", tag)
+            nc.vector.scalar_tensor_tensor(kept[c, t][:], tanh_h[c, t][:], 1.0, old_half[c, t][:], ALU.subtract, ALU.mult)
+
+        def put(c, t):
+            silu_h[c, t] = tile([P, CH], F32, f"silu_h{c}{t}")
+            nc.scalar.activation(silu_h[c, t][:], h_rows(c, t), ACT.Silu)
+            nc.vector.tensor_tensor(page[t][:].indirect(piece(n3_t, c)), kept[c, t][:], silu_h[c, t][:], ALU.add)
+
+        out_rows = out_0.rearrange("(p t) u -> t p u", t=PACK)
+        o_rows = tile([P, PACK, U], BF16, "o_rows")
+        for t in range(2):
+            for c in range(NCH):
+                fetch_old(c, t)
+        d2[0] = tile([P, PACK, CH], F32, "d2_0")
+        dd[0] = tile([P, PACK, CH], F32, "dd_0")
+        th[0] = tagged([P, PACK, CH], F32, "th_0", "ring_b")
+        for t in range(PACK):
+            evac(t)
+            y_product(t)
+            diff(0, t)
+            if t > 0:
+                tanh_rows(0, t - 1, t)
+                z_row(0, t - 1)
+        tanh_rows(0, PACK - 1, PACK)
+        z_row(0, PACK - 1)
+        h_product(0, nc.vector.tensor_copy)
+        d2[1] = tagged([P, PACK, CH], F32, "d2_1", "ring_b")
+        dd[1] = tile([P, PACK, CH], F32, "dd_1")
+        for t in range(PACK):
+            diff(1, t)
+        keep(0, 0, "kept00")
+        keep(0, 1, "kept01")
+        put(0, 0)
+        th[1] = tagged([P, PACK, CH], F32, "th_1", "ring_c00")
+        for t in range(PACK):
+            if t % 2 == 0:
+                tanh_rows(1, t, t + 2)
+            z_row(1, t)
+        fetch_old(0, 2)
+        keep(0, 2, "ring_c00")
+        put(0, 1)
+        h_product(1, nc.scalar.copy)
+        fetch_old(0, 3)
+        keep(0, 3, "woven1")
+        put(0, 2)
+        keep(1, 0, "kept10")
+        put(0, 3)
+        for t in range(1, PACK):
+            if t >= 2:
+                fetch_old(1, t)
+            keep(1, t, f"kept1{t}")
+            put(1, t - 1)
+        put(1, PACK - 1)
+        for t in range(PACK):
+            nc.sync.dma_start(out_rows[t], page[t][:])
+            if t < PACK - 1:
+                nc.scalar.copy(o_rows[:, t, :], page[t][:])
+        half = U // 2
+        quarter = U // 4
+        o_woven = [tile([P, quarter, PACK], BF16, f"o_woven{i}") for i in range(4)]
+        o_w = tile([P, U], U32, "o_w")
+        o_s = tile([P, U], U8, "o_s")
+        words_out = out_1[0].rearrange("p n t -> p (n t)").bitcast(I32)
+        copies = (nc.vector.tensor_copy, nc.scalar.copy)
+        for i in range(2):
+            cols = slice(half * i, half * (i + 1))
+            copies[i](o_rows[:, PACK - 1, cols], page[PACK - 1][:, cols])
+        for i in (0, 2, 1, 3):
+            weave(copies[i // 2], o_woven[i][:], o_rows[:, :, quarter * i : quarter * (i + 1)])
+        for i in (0, 2, 1, 3):
+            cols = slice(quarter * i, quarter * (i + 1))
+            nc.vector.quantize_mx(out=o_w[:, cols].bitcast(FP8X4), scales=o_s[:, cols], in_=o_woven[i][:].rearrange("p c t -> p (c t)"))
+            nc.sync.dma_start(words_out[:, cols], o_w[:, cols].bitcast(I32))
+        for q in range(4):
+            queue = nc.sync if q % 2 == 0 else nc.scalar
+            queue.dma_start(out_2[0, 4 * q : 4 * q + 4, :].bitcast(I32), o_s[32 * q : 32 * q + 4, :].bitcast(I32))

@@ -56,86 +56,86 @@ def tile_picked_twkeyjointbpaget_none_po_kernel(
             for q in range(4):
                 queue.dma_start(dst[32 * q : 32 * q + 4, :].bitcast(I32), src[0, 4 * q : 4 * q + 4, :].bitcast(I32))
 
-        ds_win = tile([P, G], U8, "ds_win")
+        ds_win = tagged([P, G], U8, "ds_win", "slot4")
         xs_win = tile([P, T], U8, "xs_win")
-        dk_plane = tile([P, H], U8, "dk_plane")
-        w1s_raw = tile([P, H], U8, "w1s_raw")
-        zero(nc.gpsimd, ds_win)
-        zero(nc.vector, xs_win)
-        zero(nc.vector, dk_plane)
-        zero(nc.gpsimd, w1s_raw)
-        w2s_raw = tile([P, N], U8, "w2s_raw")
-        zero(nc.gpsimd, w2s_raw)
+        planes = tile([P, 3, S], U8, "planes")
+        zero(nc.gpsimd, xs_win)
+        zero(nc.vector, ds_win)
+        zero(nc.vector, planes)
 
-        k1_t = load_list(k1, "k1_t")
         two_t = load_list(two, "two_t")
         offs_t = load_list(offs, "offs_t")
+        k1_t = load_list(k1, "k1_t")
+        nc.sync.dma_start(xs_win[0:P:8, :].bitcast(I32), x_scales[0].bitcast(I32))
+        nc.sync.dma_start(ds_win[0:P:8, :].bitcast(I32), d_scales[0].bitcast(I32))
+        dw_win = tagged([P, G], U32, "dw_win", "slot5")
+        nc.sync.dma_start(dw_win[:].bitcast(I32), d_words[0].rearrange("p n t -> p (n t)").bitcast(I32))
         n2_t = load_list(n2, "n2_t")
         n1_t = load_list(n1, "n1_t")
+        xw_win = tagged([P, T], U32, "xw_win", "slot3")
+        nc.sync.dma_start(xw_win[:].bitcast(I32), x_words[0].rearrange("p n t -> p (n t)").bitcast(I32))
         n3_t = load_list(n3, "n3_t")
         w1_raw = tile([P, 2 * H], U8, "w1_raw")
-        nc.sync.dma_start(w1_raw[:].bitcast(I32), w1_words[0].bitcast(I32))
-        dw_win = tile([P, G], U32, "dw_win")
-        nc.sync.dma_start(dw_win[:].bitcast(I32), d_words[0].rearrange("p n t -> p (n t)").bitcast(I32))
-        nc.sync.dma_start(ds_win[0:P:8, :].bitcast(I32), d_scales[0].bitcast(I32))
-        load_scale_rows(nc.sync, xs_win, x_scales)
-        mem_rows = mem.rearrange("(p t) u -> t p u", t=PACK)
-        page = [tile([P, U], F32, "page0"), tile([P, U], F32, "page1")]
-        nc.sync.dma_start(page[0][:], mem_rows[0])
-        xw_win = tile([P, T], U32, "xw_win")
-        nc.sync.dma_start(xw_win[:].bitcast(I32), x_words[0].rearrange("p n t -> p (n t)").bitcast(I32))
-        nc.sync.dma_start(page[1][:], mem_rows[1])
+        nc.gpsimd.dma_start(w1_raw[:].bitcast(I32), w1_words[0].bitcast(I32))
+        w2_raw = tile([P, 2 * N], U8, "w2_raw")
+        nc.gpsimd.dma_start(w2_raw[:].bitcast(I32), w2_words[0].bitcast(I32))
+        gn_t = tile([P, PACK], F32, "gn_t")
+        nc.gpsimd.dma_start(gn_t[:], gn.rearrange("(p t) o -> p (t o)", t=PACK))
 
-        dk_s = tagged([P, H], U8, "dk_s", "slot2")
-        nc.vector.tensor_copy(dk_s[:], ds_win[:].indirect(k1_t[:]))
-        dk_s_dealt = tagged([P, H], U8, "dk_s_dealt", "slot0")
-        nc.vector.tensor_copy(dealt(dk_s_dealt[:]), natural(dk_s[:]))
+        picked_s = tagged([P, 3, S], U8, "picked_s", "slot0")
+        nc.vector.tensor_copy(picked_s[:, 1, :], xs_win[:].indirect(two_t[:]))
+        nc.vector.tensor_copy(picked_s[:, 2, :], xs_win[:].indirect(offs_t[:]))
+        nc.vector.tensor_copy(picked_s[:, 0, :], ds_win[:].indirect(k1_t[:]))
         for r in range(4):
-            nc.scalar.dma_start(dk_plane[r:P:32, :].bitcast(I32), dk_s_dealt[8 * r : P : 32, :].bitcast(I32))
-        dk_w = tile([P, H], U32, "dk_w")
+            nc.sync.dma_start(planes[r:P:32].rearrange("p a s -> p (a s)").bitcast(I32),
+                              picked_s[8 * r : P : 32].rearrange("p a s -> p (a s)").bitcast(I32))
+        xt_s = planes[:, 1, :]
+        xq_s = planes[:, 2, :]
+        dk_w = tagged([P, H], U32, "dk_w", "slot4")
         nc.vector.tensor_copy(dk_w[:], dw_win[:].indirect(k1_t[:]))
         dk_w_dealt = tagged([P, H], U32, "dk_w_dealt", "slot1")
         nc.vector.tensor_copy(dealt(dk_w_dealt[:]), natural(dk_w[:]))
-        xt_s = tagged([P, S], U8, "xt_s", "slot2")
-        nc.vector.tensor_copy(xt_s[:], xs_win[:].indirect(two_t[:]))
-        xt_w = tagged([P, S], U32, "xt_w", "slot3")
+        xt_w = tagged([P, S], U32, "xt_w", "slot2")
         nc.vector.tensor_copy(xt_w[:], xw_win[:].indirect(two_t[:]))
-        xq_s = tagged([P, S], U8, "xq_s", "slot0")
-        nc.vector.tensor_copy(xq_s[:], xs_win[:].indirect(offs_t[:]))
-        xq_w = tile([P, S], U32, "xq_w")
+        dk_plane = tile([P, H], U8, "dk_plane")
+        nc.vector.tensor_copy(dealt(dk_plane[:]), natural(planes[:, 0, :]))
+        xq_w = tagged([P, S], U32, "xq_w", "slot0")
         nc.vector.tensor_copy(xq_w[:], xw_win[:].indirect(offs_t[:]))
 
-        load_scale_rows(nc.gpsimd, w1s_raw, w1_scales)
-        gn_t = tile([P, PACK], F32, "gn_t")
-        nc.sync.dma_start(gn_t[:], gn.rearrange("(p t) o -> p (t o)", t=PACK))
-        w2_raw = tile([P, 2 * N], U8, "w2_raw")
-        nc.sync.dma_start(w2_raw[:].bitcast(I32), w2_words[0].bitcast(I32))
-        load_scale_rows(nc.gpsimd, w2s_raw, w2_scales)
+        mem_rows = mem.rearrange("(p t) u -> t p u", t=PACK)
+        page = []
+
+        def load_page(tag):
+            t = len(page)
+            page.append(tagged([P, U], F32, f"page{t}", tag))
+            nc.sync.dma_start(page[t][:], mem_rows[t])
+
+
+        ws_raw = tagged([P, 2, H], U8, "ws_raw", "slot5")
+        zero(nc.gpsimd, ws_raw)
+        load_scale_rows(nc.sync, ws_raw[:, 0, :], w1_scales)
+        load_scale_rows(nc.sync, ws_raw[:, 1, :], w2_scales)
         w1_dealt = tile([P, 2 * H], U8, "w1_dealt")
         nc.scalar.copy(dealt(w1_dealt[:].bitcast(U16)), natural(w1_raw[:].bitcast(U16)))
         w1s = tile([P, H], U8, "w1s")
-        nc.gpsimd.tensor_copy(dealt(w1s[:]), natural(w1s_raw[:]))
+        nc.vector.tensor_copy(dealt(w1s[:]), natural(ws_raw[:, 0, :]))
         d_ps, y_ps = [], []
         for t in range(PACK):
             d_ps.append(psum.tile([P, S], F32, name=f"d_ps{t}", tag=f"bank{t}"))
             cols = slice(P * t, P * (t + 1))
             nc.tensor.matmul_mx(out=d_ps[t][:], lhsT=dk_w_dealt[:, cols].bitcast(FP8X4), lhsT_scale=dk_plane[:, cols],
-                                rhs=xt_w[:].bitcast(FP8X4), rhs_scale=xt_s[:], start=True, stop=True)
+                                rhs=xt_w[:].bitcast(FP8X4), rhs_scale=xt_s, start=True, stop=True)
         w2_dealt = tile([P, 2 * N], U8, "w2_dealt")
         nc.scalar.copy(dealt(w2_dealt[:].bitcast(U16)), natural(w2_raw[:].bitcast(U16)))
-        w2s = tile([P, N], U8, "w2s")
-        nc.gpsimd.tensor_copy(dealt(w2s[:]), natural(w2s_raw[:]))
 
-        page.append(tagged([P, U], F32, "page2", "slot1"))
-        nc.sync.dma_start(page[2][:], mem_rows[2])
-        page.append(tagged([P, U], F32, "page3", "slot3"))
-        nc.sync.dma_start(page[3][:], mem_rows[3])
+        for tag in ("slot4", "slot2", "slot1", "slot3"):
+            load_page(tag)
 
         def y_product(t):
             y_ps.append(psum.tile([P, S], F32, name=f"y_ps{t}", tag=f"bank{t}"))
             nc.tensor.matmul_mx(out=y_ps[t][:], lhsT=w1_dealt[:, 2 * P * t : 2 * P * (t + 1)].bitcast(FP4X4),
                                 lhsT_scale=w1s[:, P * t : P * (t + 1)],
-                                rhs=xq_w[:].bitcast(FP8X4), rhs_scale=xq_s[:], start=True, stop=True)
+                                rhs=xq_w[:].bitcast(FP8X4), rhs_scale=xq_s, start=True, stop=True)
 
         d_sb = [tile([P, S], F32, f"d_sb{t}") for t in range(PACK)]
         d2, dd, th = {}, {}, {}
@@ -152,7 +152,7 @@ def tile_picked_twkeyjointbpaget_none_po_kernel(
             engine_copy(dst.rearrange("p (c i) t -> p c t i", i=4), src.rearrange("p t (c i) -> p c t i", i=4))
 
         def evac(t):
-            if t < 3:
+            if t % 2 == 0:
                 nc.scalar.copy(d_sb[t][:], d_ps[t][:])
             else:
                 nc.vector.tensor_copy(d_sb[t][:], d_ps[t][:])
@@ -201,10 +201,7 @@ def tile_picked_twkeyjointbpaget_none_po_kernel(
 
         out_rows = out_0.rearrange("(p t) u -> t p u", t=PACK)
         o_rows = tile([P, PACK, U], BF16, "o_rows")
-        for t in range(2):
-            for c in range(NCH):
-                fetch_old(c, t)
-        d2[0] = tile([P, PACK, CH], F32, "d2_0")
+        d2[0] = tagged([P, PACK, CH], F32, "d2_0", "ring_d")
         dd[0] = tile([P, PACK, CH], F32, "dd_0")
         th[0] = tagged([P, PACK, CH], F32, "th_0", "ring_b")
         for t in range(PACK):
@@ -216,12 +213,16 @@ def tile_picked_twkeyjointbpaget_none_po_kernel(
                 z_row(0, t - 1)
         tanh_rows(0, PACK - 1, PACK)
         z_row(0, PACK - 1)
+        w2s = tagged([P, N], U8, "w2s", "ring_d")
+        nc.vector.tensor_copy(dealt(w2s[:]), natural(ws_raw[:, 1, :]))
         h_product(0, nc.vector.tensor_copy)
+        fetch_old(0, 0)
         d2[1] = tagged([P, PACK, CH], F32, "d2_1", "ring_b")
         dd[1] = tile([P, PACK, CH], F32, "dd_1")
         for t in range(PACK):
             diff(1, t)
         keep(0, 0, "kept00")
+        fetch_old(0, 1)
         keep(0, 1, "kept01")
         put(0, 0)
         th[1] = tagged([P, PACK, CH], F32, "th_1", "ring_c00")
@@ -236,11 +237,11 @@ def tile_picked_twkeyjointbpaget_none_po_kernel(
         fetch_old(0, 3)
         keep(0, 3, "woven1")
         put(0, 2)
+        fetch_old(1, 0)
         keep(1, 0, "kept10")
         put(0, 3)
         for t in range(1, PACK):
-            if t >= 2:
-                fetch_old(1, t)
+            fetch_old(1, t)
             keep(1, t, f"kept1{t}")
             put(1, t - 1)
         put(1, PACK - 1)
@@ -250,19 +251,19 @@ def tile_picked_twkeyjointbpaget_none_po_kernel(
                 nc.scalar.copy(o_rows[:, t, :], page[t][:])
         half = U // 2
         quarter = U // 4
-        o_woven = [tile([P, quarter, PACK], BF16, f"o_woven{i}") for i in range(4)]
         o_w = tile([P, U], U32, "o_w")
         o_s = tile([P, U], U8, "o_s")
         words_out = out_1[0].rearrange("p n t -> p (n t)").bitcast(I32)
-        copies = (nc.vector.tensor_copy, nc.scalar.copy)
-        for i in range(2):
-            cols = slice(half * i, half * (i + 1))
-            copies[i](o_rows[:, PACK - 1, cols], page[PACK - 1][:, cols])
-        for i in (0, 2, 1, 3):
-            weave(copies[i // 2], o_woven[i][:], o_rows[:, :, quarter * i : quarter * (i + 1)])
-        for i in (0, 2, 1, 3):
-            cols = slice(quarter * i, quarter * (i + 1))
-            nc.vector.quantize_mx(out=o_w[:, cols].bitcast(FP8X4), scales=o_s[:, cols], in_=o_woven[i][:].rearrange("p c t -> p (c t)"))
+        pieces = ((0, half, nc.vector.tensor_copy), (half, quarter, nc.scalar.copy), (half + quarter, quarter, nc.scalar.copy))
+        o_woven = []
+        for start, width, copy in pieces:
+            cols = slice(start, start + width)
+            o_woven.append(tile([P, width, PACK], BF16, f"o_woven{start}"))
+            copy(o_rows[:, PACK - 1, cols], page[PACK - 1][:, cols])
+            weave(copy, o_woven[-1][:], o_rows[:, :, cols])
+        for (start, width, copy), woven in zip(pieces, o_woven):
+            cols = slice(start, start + width)
+            nc.vector.quantize_mx(out=o_w[:, cols].bitcast(FP8X4), scales=o_s[:, cols], in_=woven[:].rearrange("p c t -> p (c t)"))
             nc.sync.dma_start(words_out[:, cols], o_w[:, cols].bitcast(I32))
         for q in range(4):
             queue = nc.sync if q % 2 == 0 else nc.scalar

@@ -46,11 +46,8 @@ def tile_picked_twkeyjointbpaget_none_po_kernel(
         def zero(engine, t):
             engine.memset(t[:].bitcast(I32), 0)
 
-        def dealt(ap):
-            return ap.rearrange("p (t m) -> p m t", t=PACK)
-
-        def natural(ap):
-            return ap.rearrange("p (m t) -> p m t", t=PACK)
+        def deal(copy, dst, src, per_line):
+            copy(dst.rearrange("p (t c i) -> p c t i", t=PACK, i=per_line), src.rearrange("p (c i t) -> p c t i", t=PACK, i=per_line))
 
         def load_scale_rows(queue, dst, src):
             for q in range(4):
@@ -94,11 +91,11 @@ def tile_picked_twkeyjointbpaget_none_po_kernel(
         dk_w = tagged([P, H], U32, "dk_w", "slot4")
         nc.vector.tensor_copy(dk_w[:], dw_win[:].indirect(k1_t[:]))
         dk_w_dealt = tagged([P, H], U32, "dk_w_dealt", "slot1")
-        nc.vector.tensor_copy(dealt(dk_w_dealt[:]), natural(dk_w[:]))
+        deal(nc.vector.tensor_copy, dk_w_dealt[:], dk_w[:], 4)
         xt_w = tagged([P, S], U32, "xt_w", "slot2")
         nc.vector.tensor_copy(xt_w[:], xw_win[:].indirect(two_t[:]))
         dk_plane = tile([P, H], U8, "dk_plane")
-        nc.vector.tensor_copy(dealt(dk_plane[:]), natural(planes[:, 0, :]))
+        deal(nc.vector.tensor_copy, dk_plane[:], planes[:, 0, :], 16)
         xq_w = tagged([P, S], U32, "xq_w", "slot0")
         nc.vector.tensor_copy(xq_w[:], xw_win[:].indirect(offs_t[:]))
 
@@ -116,17 +113,17 @@ def tile_picked_twkeyjointbpaget_none_po_kernel(
         load_scale_rows(nc.sync, ws_raw[:, 0, :], w1_scales)
         load_scale_rows(nc.sync, ws_raw[:, 1, :], w2_scales)
         w1_dealt = tile([P, 2 * H], U8, "w1_dealt")
-        nc.scalar.copy(dealt(w1_dealt[:].bitcast(U16)), natural(w1_raw[:].bitcast(U16)))
+        deal(nc.scalar.copy, w1_dealt[:].bitcast(U16), w1_raw[:].bitcast(U16), 8)
         w1s = tile([P, H], U8, "w1s")
-        nc.vector.tensor_copy(dealt(w1s[:]), natural(ws_raw[:, 0, :]))
+        deal(nc.vector.tensor_copy, w1s[:], ws_raw[:, 0, :], 16)
         d_ps, y_ps = [], []
         for t in range(PACK):
             d_ps.append(psum.tile([P, S], F32, name=f"d_ps{t}", tag=f"bank{t}"))
-            cols = slice(P * t, P * (t + 1))
-            nc.tensor.matmul_mx(out=d_ps[t][:], lhsT=dk_w_dealt[:, cols].bitcast(FP8X4), lhsT_scale=dk_plane[:, cols],
+            rows = slice(P * t, P * (t + 1))
+            nc.tensor.matmul_mx(out=d_ps[t][:], lhsT=dk_w_dealt[:, rows].bitcast(FP8X4), lhsT_scale=dk_plane[:, rows],
                                 rhs=xt_w[:].bitcast(FP8X4), rhs_scale=xt_s, start=True, stop=True)
         w2_dealt = tile([P, 2 * N], U8, "w2_dealt")
-        nc.scalar.copy(dealt(w2_dealt[:].bitcast(U16)), natural(w2_raw[:].bitcast(U16)))
+        deal(nc.scalar.copy, w2_dealt[:].bitcast(U16), w2_raw[:].bitcast(U16), 8)
 
         for tag in ("slot4", "slot2", "slot1", "slot3"):
             load_page(tag)
@@ -214,7 +211,7 @@ def tile_picked_twkeyjointbpaget_none_po_kernel(
         tanh_rows(0, PACK - 1, PACK)
         z_row(0, PACK - 1)
         w2s = tagged([P, N], U8, "w2s", "ring_d")
-        nc.vector.tensor_copy(dealt(w2s[:]), natural(ws_raw[:, 1, :]))
+        deal(nc.vector.tensor_copy, w2s[:], ws_raw[:, 1, :], 16)
         h_product(0, nc.vector.tensor_copy)
         fetch_old(0, 0)
         d2[1] = tagged([P, PACK, CH], F32, "d2_1", "ring_b")
@@ -249,22 +246,35 @@ def tile_picked_twkeyjointbpaget_none_po_kernel(
             nc.sync.dma_start(out_rows[t], page[t][:])
             if t < PACK - 1:
                 nc.scalar.copy(o_rows[:, t, :], page[t][:])
-        half = U // 2
         quarter = U // 4
         o_w = tile([P, U], U32, "o_w")
         o_s = tile([P, U], U8, "o_s")
         words_out = out_1[0].rearrange("p n t -> p (n t)").bitcast(I32)
-        pieces = ((0, half, nc.vector.tensor_copy), (half, quarter, nc.scalar.copy), (half + quarter, quarter, nc.scalar.copy))
-        o_woven = []
-        for start, width, copy in pieces:
-            cols = slice(start, start + width)
-            o_woven.append(tile([P, width, PACK], BF16, f"o_woven{start}"))
-            copy(o_rows[:, PACK - 1, cols], page[PACK - 1][:, cols])
-            weave(copy, o_woven[-1][:], o_rows[:, :, cols])
-        for (start, width, copy), woven in zip(pieces, o_woven):
-            cols = slice(start, start + width)
-            nc.vector.quantize_mx(out=o_w[:, cols].bitcast(FP8X4), scales=o_s[:, cols], in_=woven[:].rearrange("p c t -> p (c t)"))
-            nc.sync.dma_start(words_out[:, cols], o_w[:, cols].bitcast(I32))
+        o_woven = [tile([P, quarter, PACK], BF16, f"o_woven{i}") for i in range(4)]
+
+        def cols(i):
+            return slice(quarter * i, quarter * (i + 1))
+
+        def round_last(copy, i):
+            copy(o_rows[:, PACK - 1, cols(i)], page[PACK - 1][:, cols(i)])
+
+        def weave_out(copy, i):
+            weave(copy, o_woven[i][:], o_rows[:, :, cols(i)])
+
+        def quantise_out(i):
+            nc.vector.quantize_mx(out=o_w[:, cols(i)].bitcast(FP8X4), scales=o_s[:, cols(i)],
+                                  in_=o_woven[i][:].rearrange("p c t -> p (c t)"))
+            nc.sync.dma_start(words_out[:, cols(i)], o_w[:, cols(i)].bitcast(I32))
+
+        for i in (0, 1):
+            round_last(nc.vector.tensor_copy, i)
+        for i in (2, 3):
+            round_last(nc.scalar.copy, i)
+            weave_out(nc.scalar.copy, i)
+        for i in (0, 1):
+            weave_out(nc.vector.tensor_copy, i)
+        for i in (0, 2, 1, 3):
+            quantise_out(i)
         for q in range(4):
             queue = nc.sync if q % 2 == 0 else nc.scalar
             queue.dma_start(out_2[0, 4 * q : 4 * q + 4, :].bitcast(I32), o_s[32 * q : 32 * q + 4, :].bitcast(I32))

@@ -116,6 +116,9 @@ def tile_picked_twkeyjointbpaget_none_po_kernel(
         deal(nc.scalar.copy, w1_dealt[:].bitcast(U16), w1_raw[:].bitcast(U16), 8)
         w1s = tile([P, H], U8, "w1s")
         deal(nc.vector.tensor_copy, w1s[:], ws_raw[:, 0, :], 16)
+        warm = tile([P, 1], F32, "warm")
+        nc.scalar.activation(warm[:], gn_t[:, 0:1], ACT.Silu)
+
         d_ps, y_ps = [], []
         for t in range(PACK):
             d_ps.append(psum.tile([P, S], F32, name=f"d_ps{t}", tag=f"bank{t}"))

from contextlib import ExitStack

import concourse.mybir as mybir

K, T, S, N, H, G, U = 512, 2048, 512, 512, 512, 2048, 1024
FLOPS = 3 * 2 * 512 * 512 * 512

F32 = mybir.dt.float32
BF16 = mybir.dt.bfloat16
I32 = mybir.dt.int32
U32 = mybir.dt.uint32
U16 = mybir.dt.uint16
U8 = mybir.dt.uint8
FP8X4 = mybir.dt.float8_e4m3fn_x4
FP4X4 = mybir.dt.float4_e2m1fn_x4
ACT = mybir.ActivationFunctionType
ALU = mybir.AluOpType

P = 128
PACK = 4
CH = 256
NCH = S // CH


def tile_picked_twkeyjointbpaget_none_po_kernel(
    tc, x_words, x_scales, w1_words, w1_scales, d_words, d_scales, gn, w2_words, w2_scales, mem,
    offs, k1, two, n1, n2, n3, out_0, out_1, out_2,
):
    nc = tc.nc
    with ExitStack() as ctx:
        lists = ctx.enter_context(tc.tile_pool(name="lists", bufs=1))
        sb = ctx.enter_context(tc.tile_pool(name="sb", bufs=1))
        psum = ctx.enter_context(tc.psum_pool(name="psum", bufs=1))

        def tile(shape, dtype, name):
            return sb.tile(shape, dtype, name=name, align_bytes=64)

        def tagged(shape, dtype, name, tag):
            return sb.tile(shape, dtype, name=name, tag=tag, align_bytes=64)

        def load_list(src, name):
            t = lists.tile([P, S // 16], U16, name=name)
            nc.sync.dma_start(t[:], src)
            return t

        def zero(engine, t):
            engine.memset(t[:].bitcast(I32), 0)

        def deal(copy, dst, src, per_line):
            copy(dst.rearrange("p (t c i) -> p c t i", t=PACK, i=per_line), src.rearrange("p (c i t) -> p c t i", t=PACK, i=per_line))

        def load_scale_rows(queue, dst, src):
            for q in range(4):
                queue.dma_start(dst[32 * q : 32 * q + 4, :].bitcast(I32), src[0, 4 * q : 4 * q + 4, :].bitcast(I32))

        ds_win = tagged([P, G], U8, "ds_win", "slot4")
        xs_win = tile([P, T], U8, "xs_win")
        planes = tile([P, 3, S], U8, "planes")
        zero(nc.gpsimd, xs_win)
        zero(nc.vector, ds_win)
        zero(nc.vector, planes)

        two_t = load_list(two, "two_t")
        offs_t = load_list(offs, "offs_t")
        k1_t = load_list(k1, "k1_t")
        nc.sync.dma_start(xs_win[0:P:8, :].bitcast(I32), x_scales[0].bitcast(I32))
        nc.sync.dma_start(ds_win[0:P:8, :].bitcast(I32), d_scales[0].bitcast(I32))
        dw_win = tagged([P, G], U32, "dw_win", "slot5")
        nc.sync.dma_start(dw_win[:].bitcast(I32), d_words[0].rearrange("p n t -> p (n t)").bitcast(I32))
        n2_t = load_list(n2, "n2_t")
        n1_t = load_list(n1, "n1_t")
        xw_win = tagged([P, T], U32, "xw_win", "slot3")
        nc.sync.dma_start(xw_win[:].bitcast(I32), x_words[0].rearrange("p n t -> p (n t)").bitcast(I32))
        n3_t = load_list(n3, "n3_t")
        w1_raw = tile([P, 2 * H], U8, "w1_raw")
        nc.gpsimd.dma_start(w1_raw[:].bitcast(I32), w1_words[0].bitcast(I32))
        w2_raw = tile([P, 2 * N], U8, "w2_raw")
        nc.gpsimd.dma_start(w2_raw[:].bitcast(I32), w2_words[0].bitcast(I32))
        gn_t = tile([P, PACK], F32, "gn_t")
        nc.gpsimd.dma_start(gn_t[:], gn.rearrange("(p t) o -> p (t o)", t=PACK))

        picked_s = tagged([P, 3, S], U8, "picked_s", "slot0")
        nc.vector.tensor_copy(picked_s[:, 1, :], xs_win[:].indirect(two_t[:]))
        nc.vector.tensor_copy(picked_s[:, 2, :], xs_win[:].indirect(offs_t[:]))
        nc.vector.tensor_copy(picked_s[:, 0, :], ds_win[:].indirect(k1_t[:]))
        for r in range(4):
            nc.sync.dma_start(planes[r:P:32].rearrange("p a s -> p (a s)").bitcast(I32),
                              picked_s[8 * r : P : 32].rearrange("p a s -> p (a s)").bitcast(I32))
        xt_s = planes[:, 1, :]
        xq_s = planes[:, 2, :]
        dk_w = tagged([P, H], U32, "dk_w", "slot4")
        nc.vector.tensor_copy(dk_w[:], dw_win[:].indirect(k1_t[:]))
        dk_w_dealt = tagged([P, H], U32, "dk_w_dealt", "slot1")
        deal(nc.vector.tensor_copy, dk_w_dealt[:], dk_w[:], 4)
        xt_w = tagged([P, S], U32, "xt_w", "slot2")
        nc.vector.tensor_copy(xt_w[:], xw_win[:].indirect(two_t[:]))
        dk_plane = tile([P, H], U8, "dk_plane")
        deal(nc.vector.tensor_copy, dk_plane[:], planes[:, 0, :], 16)
        xq_w = tagged([P, S], U32, "xq_w", "slot0")
        nc.vector.tensor_copy(xq_w[:], xw_win[:].indirect(offs_t[:]))

        mem_rows = mem.rearrange("(p t) u -> t p u", t=PACK)
        page = []

        def load_page(tag):
            t = len(page)
            page.append(tagged([P, U], F32, f"page{t}", tag))
            nc.sync.dma_start(page[t][:], mem_rows[t])


        ws_raw = tagged([P, 2, H], U8, "ws_raw", "slot5")
        zero(nc.gpsimd, ws_raw)
        load_scale_rows(nc.sync, ws_raw[:, 0, :], w1_scales)
        load_scale_rows(nc.sync, ws_raw[:, 1, :], w2_scales)
        w1_dealt = tile([P, 2 * H], U8, "w1_dealt")
        deal(nc.scalar.copy, w1_dealt[:].bitcast(U16), w1_raw[:].bitcast(U16), 8)
        w1s = tile([P, H], U8, "w1s")
        deal(nc.vector.tensor_copy, w1s[:], ws_raw[:, 0, :], 16)
        warm = tile([P, 1], F32, "warm")
        nc.scalar.activation(warm[:], gn_t[:, 0:1], ACT.Silu)

        d_ps, y_ps = [], []
        for t in range(PACK):
            d_ps.append(psum.tile([P, S], F32, name=f"d_ps{t}", tag=f"bank{t}"))
            rows = slice(P * t, P * (t + 1))
            nc.tensor.matmul_mx(out=d_ps[t][:], lhsT=dk_w_dealt[:, rows].bitcast(FP8X4), lhsT_scale=dk_plane[:, rows],
                                rhs=xt_w[:].bitcast(FP8X4), rhs_scale=xt_s, start=True, stop=True)
        w2_dealt = tile([P, 2 * N], U8, "w2_dealt")
        deal(nc.scalar.copy, w2_dealt[:].bitcast(U16), w2_raw[:].bitcast(U16), 8)

        for tag in ("slot4", "slot2", "slot1", "slot3"):
            load_page(tag)

        def y_product(t):
            y_ps.append(psum.tile([P, S], F32, name=f"y_ps{t}", tag=f"bank{t}"))
            nc.tensor.matmul_mx(out=y_ps[t][:], lhsT=w1_dealt[:, 2 * P * t : 2 * P * (t + 1)].bitcast(FP4X4),
                                lhsT_scale=w1s[:, P * t : P * (t + 1)],
                                rhs=xq_w[:].bitcast(FP8X4), rhs_scale=xq_s, start=True, stop=True)

        d_sb = [tile([P, S], F32, f"d_sb{t}") for t in range(PACK)]
        d2, dd, th = {}, {}, {}
        z_rows = [tile([P, PACK, CH], BF16, f"z_rows{c}") for c in range(NCH)]
        z_woven = [tagged([P, CH, PACK], BF16, f"z_woven{c}", f"woven{c}") for c in range(NCH)]
        z_w = [tile([P, CH], U32, f"z_w{c}") for c in range(NCH)]
        z_s = [tile([P, CH], U8, f"z_s{c}") for c in range(NCH)]
        old_half, silu_h, tanh_h, kept = {}, {}, {}, {}

        def piece(lst, c):
            return lst[:, c * CH // 16 : (c + 1) * CH // 16]

        def weave(engine_copy, dst, src):
            engine_copy(dst.rearrange("p (c i) t -> p c t i", i=4), src.rearrange("p t (c i) -> p c t i", i=4))

        def evac(t):
            if t % 2 == 0:
                nc.scalar.copy(d_sb[t][:], d_ps[t][:])
            else:
                nc.vector.tensor_copy(d_sb[t][:], d_ps[t][:])

        def diff(c, t):
            nc.scalar.activation(d2[c][:, t, :], d_sb[t][:].indirect(piece(n2_t, c)), ACT.Copy)
            nc.vector.tensor_tensor(dd[c][:, t, :], d_sb[t][:].indirect(piece(n1_t, c)), d2[c][:, t, :], ALU.subtract)

        def tanh_rows(c, t0, t1):
            nc.scalar.activation(th[c][:, t0:t1, :], dd[c][:, t0:t1, :], ACT.Tanh, scale=0.0625)

        def z_row(c, t):
            nc.vector.scalar_tensor_tensor(z_rows[c][:, t, :], y_ps[t][:, c * CH : (c + 1) * CH], gn_t[:, t : t + 1],
                                           th[c][:, t, :], ALU.mult, ALU.mult)

        def fetch_old(c, t):
            old_half[c, t] = tagged([P, CH], F32, f"old_half{c}{t}", f"old{c}{t % 2}")
            nc.scalar.activation(old_half[c, t][:], page[t][:].indirect(piece(n3_t, c)), ACT.Copy, scale=-0.5)

        h_ps = {}

        def h_product(c, copy):
            weave(copy, z_woven[c][:], z_rows[c][:])
            nc.vector.quantize_mx(out=z_w[c][:].bitcast(FP8X4), scales=z_s[c][:], in_=z_woven[c][:].rearrange("p c t -> p (c t)"))
            for u in range(2):
                h_ps[c, u] = psum.tile([P, 2, CH], F32, name=f"h_ps{c}{u}", tag=f"bank{4 + 2 * c + u}")
                for e in range(2):
                    t = 2 * u + e
                    nc.tensor.matmul_mx(out=h_ps[c, u][:, e, :], lhsT=w2_dealt[:, 2 * P * t : 2 * P * (t + 1)].bitcast(FP4X4),
                                        lhsT_scale=w2s[:, P * t : P * (t + 1)], rhs=z_w[c][:].bitcast(FP8X4), rhs_scale=z_s[c][:],
                                        start=True, stop=True)

        def h_rows(c, t):
            return h_ps[c, t // 2][:, t % 2, :]

        def keep(c, t, tag):
            tanh_h[c, t] = tagged([P, CH], F32, f"tanh_h{c}{t}", f"ring_c{c}{t}")
            nc.scalar.activation(tanh_h[c, t][:], h_rows(c, t), ACT.Tanh, scale=0.5)
            kept[c, t] = tagged([P, CH], F32, f"kept{c}{t}", tag)
            nc.vector.scalar_tensor_tensor(kept[c, t][:], tanh_h[c, t][:], 1.0, old_half[c, t][:], ALU.subtract, ALU.mult)

        def put(c, t):
            silu_h[c, t] = tile([P, CH], F32, f"silu_h{c}{t}")
            nc.scalar.activation(silu_h[c, t][:], h_rows(c, t), ACT.Silu)
            nc.vector.tensor_tensor(page[t][:].indirect(piece(n3_t, c)), kept[c, t][:], silu_h[c, t][:], ALU.add)

        out_rows = out_0.rearrange("(p t) u -> t p u", t=PACK)
        o_rows = tile([P, PACK, U], BF16, "o_rows")
        d2[0] = tagged([P, PACK, CH], F32, "d2_0", "ring_d")
        dd[0] = tile([P, PACK, CH], F32, "dd_0")
        th[0] = tagged([P, PACK, CH], F32, "th_0", "ring_b")
        for t in range(PACK):
            evac(t)
            y_product(t)
            diff(0, t)
            if t > 0:
                tanh_rows(0, t - 1, t)
                z_row(0, t - 1)
        tanh_rows(0, PACK - 1, PACK)
        z_row(0, PACK - 1)
        w2s = tagged([P, N], U8, "w2s", "ring_d")
        deal(nc.vector.tensor_copy, w2s[:], ws_raw[:, 1, :], 16)
        h_product(0, nc.vector.tensor_copy)
        fetch_old(0, 0)
        d2[1] = tagged([P, PACK, CH], F32, "d2_1", "ring_b")
        dd[1] = tile([P, PACK, CH], F32, "dd_1")
        for t in range(PACK):
            diff(1, t)
        keep(0, 0, "kept00")
        fetch_old(0, 1)
        keep(0, 1, "kept01")
        put(0, 0)
        th[1] = tagged([P, PACK, CH], F32, "th_1", "ring_c00")
        for t in range(PACK):
            if t % 2 == 0:
                tanh_rows(1, t, t + 2)
            z_row(1, t)
        fetch_old(0, 2)
        keep(0, 2, "ring_c00")
        put(0, 1)
        h_product(1, nc.scalar.copy)
        fetch_old(0, 3)
        keep(0, 3, "woven1")
        put(0, 2)
        fetch_old(1, 0)
        keep(1, 0, "kept10")
        put(0, 3)
        for t in range(1, PACK):
            fetch_old(1, t)
            keep(1, t, f"kept1{t}")
            put(1, t - 1)
        put(1, PACK - 1)
        for t in range(PACK):
            nc.sync.dma_start(out_rows[t], page[t][:])
            if t < PACK - 1:
                nc.scalar.copy(o_rows[:, t, :], page[t][:])
        quarter = U // 4
        o_w = tile([P, U], U32, "o_w")
        o_s = tile([P, U], U8, "o_s")
        words_out = out_1[0].rearrange("p n t -> p (n t)").bitcast(I32)
        o_woven = [tile([P, quarter, PACK], BF16, f"o_woven{i}") for i in range(4)]

        def cols(i):
            return slice(quarter * i, quarter * (i + 1))

        def round_last(copy, i):
            copy(o_rows[:, PACK - 1, cols(i)], page[PACK - 1][:, cols(i)])

        def weave_out(copy, i):
            weave(copy, o_woven[i][:], o_rows[:, :, cols(i)])

        def quantise_out(i):
            nc.vector.quantize_mx(out=o_w[:, cols(i)].bitcast(FP8X4), scales=o_s[:, cols(i)],
                                  in_=o_woven[i][:].rearrange("p c t -> p (c t)"))
            nc.sync.dma_start(words_out[:, cols(i)], o_w[:, cols(i)].bitcast(I32))

        for i in (0, 1):
            round_last(nc.vector.tensor_copy, i)
        for i in (2, 3):
            round_last(nc.scalar.copy, i)
            weave_out(nc.scalar.copy, i)
        for i in (0, 1):
            weave_out(nc.vector.tensor_copy, i)
        for i in (0, 2, 1, 3):
            quantise_out(i)
        for q in range(4):
            queue = nc.sync if q % 2 == 0 else nc.scalar
            queue.dma_start(out_2[0, 4 * q : 4 * q + 4, :].bitcast(I32), o_s[32 * q : 32 * q + 4, :].bitcast(I32))
